import numpy as np
import ml_dtypes


def mxq(x, axis, fmt="e4m3"):
    dtype, down = {"e4m3": (ml_dtypes.float8_e4m3fn, 7), "e5m2": (ml_dtypes.float8_e5m2, 14)}[fmt]
    v = np.moveaxis(np.asarray(x, np.float32).astype(ml_dtypes.bfloat16).astype(np.float64), axis, -1)
    blocks = v.reshape(v.shape[:-1] + (-1, 32))
    amax = np.abs(blocks).max(-1, keepdims=True)
    byte = np.maximum(np.where(amax > 0, np.frexp(amax)[1] - 1 + 127, 0) - down, 1)
    scale = np.exp2(byte - 127.0)
    codes = (blocks / scale).astype(np.float32).astype(dtype).astype(np.float64)
    return np.moveaxis((codes * scale).reshape(v.shape), -1, axis)


WIDE = False


def mx_kscale(k):
    if not WIDE:
        return np.ones(k)
    levels = np.array([10, -10, 5, -5, 0])
    if k % 512:
        return np.exp2(np.random.permutation(np.resize(levels, k // 32))).repeat(32)
    a = np.empty((k // 512, 16))
    for p in range(k // 512):
        a[p, :8] = np.random.permutation(np.resize(levels, 8))
        for g in range(8):
            far = levels[np.abs(levels - a[p, g]) >= 10]
            a[p, g + 8] = far[np.random.randint(len(far))]
    return np.exp2(a.ravel()).repeat(32)


def f64(x):
    return np.asarray(x).astype(np.float64)


def striped8(idx):
    return np.asarray(idx).reshape(8, -1, 16).transpose(0, 2, 1).reshape(128, -1).astype(np.uint16)


def unstriped8(offs):
    return offs.reshape(8, 16, -1).transpose(0, 2, 1).reshape(8, -1).astype(np.int64)


def pick8(x, idx, run):
    r = np.arange(len(x))
    return x[r[:, None], idx[r % (8 * run) // run]]


E2M1 = np.array([0.0, 0.5, 1.0, 1.5, 2.0, 3.0, 4.0, 6.0, -0.0, -0.5, -1.0, -1.5, -2.0, -3.0, -4.0, -6.0])


def pack_weight(w, fmt):
    k, n = w.shape
    w = f64(np.asarray(w, np.float32).astype(ml_dtypes.bfloat16)).reshape(k // 32, 32, n)
    amax = np.abs(w).max(1)
    if fmt == "e4m3":
        byte = np.frexp(amax)[1] - 1 + 127 - 7
    else:
        mant, ex = np.frexp(amax / 6.0)
        byte = np.where(mant > 0.5, ex, ex - 1) + 127
    byte = np.clip(np.where(amax > 0, byte, 1), 1, 254)
    scaled = (w * np.exp2(127.0 - byte)[:, None, :]).reshape(k, n).astype(np.float32)
    by_word = np.ascontiguousarray(scaled.reshape(k // 512, 128, 4, n).transpose(0, 1, 3, 2))
    if fmt == "e4m3":
        words = by_word.astype(ml_dtypes.float8_e4m3fn).view(np.uint8)
    else:
        c = by_word.astype(ml_dtypes.float4_e2m1fn).view(np.uint8) & 0xF
        words = (c[..., 0::2] | (c[..., 1::2] << 4)).reshape(k // 512, 128, 2 * n)
    return np.ascontiguousarray(words), np.ascontiguousarray(byte.astype(np.uint8).reshape(k // 512, 16, n))


def unpack_weight(words, scales, fmt):
    g, _, n = scales.shape
    words = np.ascontiguousarray(words).reshape(g, 128, n, -1)
    if fmt == "e4m3":
        vals = words.view(ml_dtypes.float8_e4m3fn).astype(np.float64)
    else:
        nib = np.empty((g, 128, n, 4), np.uint8)
        nib[..., 0::2] = words & 0xF
        nib[..., 1::2] = words >> 4
        vals = E2M1[nib]
    vals = vals * np.repeat(np.exp2(scales.astype(np.float64) - 127.0), 8, axis=1)[..., None]
    return vals.transpose(0, 1, 3, 2).reshape(g * 512, n)


def softplus(v):
    return np.log(1.0 + np.exp(v))


D, T, I, Q = 512, 1024, 512, 128


def setup_inputs():
    n = np.random.standard_normal
    idx = np.stack([np.random.permutation(T)[:I] for _ in range(8)])
    idx2 = np.stack([np.random.permutation(T)[:I] for _ in range(8)])
    idx3 = np.stack([np.random.permutation(T)[:I] for _ in range(8)])
    fd = mx_kscale(D)
    keysp = pack_weight(n((D, T)) / fd[:, None], "e2m1")
    return {
        "query": (n((D, Q)) * 0.9 / np.sqrt(D) * fd[:, None]).astype(np.float32),
        "query2": (n((D, Q)) * 0.9 / np.sqrt(D) * fd[:, None]).astype(np.float32),
        "keys_words": keysp[0],
        "keys_scales": keysp[1],
        "lam": (np.random.uniform(0.6, 1.2, (Q, 1))).astype(np.float32),
        "old": (1.0 * n((Q, T))).astype(np.float32),
        "offs": striped8(idx),
        "offs2": striped8(idx2),
        "offs3": striped8(idx3),
    }


def reference(query, query2, keys_words, keys_scales, lam, old, offs, offs2, offs3):
    idx = unstriped8(offs)
    idx2 = unstriped8(offs2)
    idx3 = unstriped8(offs3)
    keysu = unpack_weight(keys_words, keys_scales, "e2m1")
    queryq = mxq(f64(query), 0, "e4m3")
    a = queryq.T @ keysu
    query2q = mxq(f64(query2), 0, "e4m3")
    b = query2q.T @ keysu
    w = pick8(a, idx, 16) / (softplus(pick8(b, idx2, 16)) + 0.5) * f64(lam)
    f1 = np.zeros((Q, T))
    f1[np.arange(Q)[:, None], idx3[np.arange(Q) % 128 // 16]] = w
    y = f64(old) + f1
    return y

@@ -1,0 +1,158 @@
+import math
+from contextlib import ExitStack
+
+import concourse.mybir as mybir
+
+D, T, I, Q = 512, 1024, 512, 128
+FLOPS = 2 * 2 * D * T * Q
+
+F32 = mybir.dt.float32
+BF16 = mybir.dt.bfloat16
+I32 = mybir.dt.int32
+U32 = mybir.dt.uint32
+U16 = mybir.dt.uint16
+U8 = mybir.dt.uint8
+FP8X4 = mybir.dt.float8_e4m3fn_x4
+FP4X4 = mybir.dt.float4_e2m1fn_x4
+ALU = mybir.AluOpType
+ACT = mybir.ActivationFunctionType
+
+P = 128
+PACK = 4
+LANES = 16
+EXP_CAP = 2.0**57
+DIVIDED = 128
+B_PIECE = 256
+A_PIECE = 512
+OUT_PIECE = 256
+
+
+def tile_attend_worthfor_lean_putold_heads_kernel(
+    tc, query, query2, keys_words, keys_scales, lam, old, offs, offs2, offs3, out
+):
+    nc = tc.nc
+    with ExitStack() as ctx:
+        pool = ctx.enter_context(tc.tile_pool(name="sbuf", bufs=1))
+        psum = ctx.enter_context(tc.psum_pool(name="psum", bufs=1))
+
+        def entries(lists, slots):
+            return lists[:, slots.start // LANES : slots.stop // LANES]
+
+        key_scales = pool.tile([P, T], U8, name="key_scales", align_bytes=64)
+        nc.vector.memset(key_scales[:].bitcast(I32), 0)
+        f1 = pool.tile([P, T], F32, name="f1")
+        nc.vector.memset(f1[:], 0.0)
+
+        raw2 = pool.tile([P, PACK, Q], F32, name="raw2")
+        nc.sync.dma_start(out=raw2[:], in_=query2.rearrange("(p j) q -> p j q", j=PACK))
+        for quad in range(4):
+            nc.scalar.dma_start(
+                out=key_scales[32 * quad : 32 * quad + 4, :].bitcast(I32),
+                in_=keys_scales[0, 4 * quad : 4 * quad + 4, :].bitcast(I32),
+            )
+        key_words = pool.tile([P, 2 * T], U8, name="key_words", align_bytes=64)
+        nc.sync.dma_start(out=key_words[:].bitcast(I32), in_=keys_words[0].bitcast(I32))
+        raw1 = pool.tile([P, PACK, Q], F32, name="raw1")
+        nc.sync.dma_start(out=raw1[:], in_=query.rearrange("(p j) q -> p j q", j=PACK))
+        list_b = pool.tile([P, I // LANES], U16, name="list_b")
+        nc.sync.dma_start(list_b[:], offs2)
+        lam_col = pool.tile([P, 1], F32, name="lam_col")
+        nc.gpsimd.dma_start(out=lam_col[:], in_=lam)
+        list_a = pool.tile([P, I // LANES], U16, name="list_a")
+        nc.sync.dma_start(list_a[:], offs)
+        list_w = pool.tile([P, I // LANES], U16, name="list_w")
+        nc.sync.dma_start(list_w[:], offs3)
+        total = pool.tile([P, T], F32, name="total")
+        nc.sync.dma_start(out=total[:], in_=old)
+
+        def quantize(raw, name):
+            grouped = pool.tile([P, Q, PACK], BF16, name=name + "_grouped", align_bytes=64)
+            nc.vector.tensor_copy(
+                out=grouped[:].rearrange("p (c i) j -> p c j i", i=4),
+                in_=raw[:].rearrange("p j (c i) -> p c j i", i=4),
+            )
+            codes = pool.tile([P, Q], U32, name=name + "_codes", align_bytes=64)
+            scales = pool.tile([P, Q], U8, name=name + "_scales", align_bytes=64)
+            nc.vector.quantize_mx(
+                out=codes[:].bitcast(FP8X4),
+                scales=scales[:],
+                in_=grouped[:].rearrange("p q j -> p (q j)"),
+            )
+            return codes, scales
+
+        def scores(codes, scales, piece, name, copy):
+            whole = pool.tile([P, T], F32, name=name)
+            for t0 in range(0, T, piece):
+                bank = psum.tile([P, piece], F32, name=f"{name}_bank{t0}")
+                nc.tensor.matmul_mx(
+                    out=bank[:],
+                    lhsT=codes[:].bitcast(FP8X4),
+                    lhsT_scale=scales[:],
+                    rhs=key_words[:, 2 * t0 : 2 * (t0 + piece)].bitcast(FP4X4),
+                    rhs_scale=key_scales[:, t0 : t0 + piece],
+                    start=True,
+                    stop=True,
+                )
+                copy(out=whole[:, t0 : t0 + piece], in_=bank[:])
+            return whole
+
+        codes2, scales2 = quantize(raw2, "q2")
+        codes1, scales1 = quantize(raw1, "q1")
+        b = scores(codes2, scales2, B_PIECE, "b", nc.scalar.copy)
+
+        half = I // 2
+        halves = [slice(0, half), slice(half, I)]
+        lam_rows = pool.tile([P, half], F32, name="lam_rows")
+        nc.vector.tensor_copy(out=lam_rows[:], in_=lam_col[:].to_broadcast([P, half]))
+
+        x = pool.tile([P, I], F32, name="x")
+        nc.scalar.activation(x[:, halves[0]], b[:].indirect(entries(list_b, halves[0])), ACT.Copy)
+        nc.vector.tensor_copy(x[:, halves[1]], b[:].indirect(entries(list_b, halves[1])))
+        e = pool.tile([P, I], F32, name="e")
+        nc.scalar.activation(e[:], x[:], ACT.Exp)
+
+        a = scores(codes1, scales1, A_PIECE, "a", nc.vector.tensor_copy)
+
+        capped = pool.tile([P, I], F32, name="capped")
+        nc.vector.tensor_scalar(capped[:], e[:], EXP_CAP, 1.0, ALU.min, ALU.add)
+
+        top = e
+        for slots in halves:
+            nc.vector.tensor_tensor(
+                top[:, slots], a[:].indirect(entries(list_a, slots)), lam_rows[:], ALU.mult
+            )
+
+        first = slice(0, DIVIDED)
+        mid = (DIVIDED + I) // 2
+        rest = [slice(DIVIDED, mid), slice(mid, I)]
+        soft = pool.tile([P, I], F32, name="soft")
+        den = pool.tile([P, I], F32, name="den")
+        for slots in rest + [first]:
+            nc.scalar.activation(soft[:, slots], capped[:, slots], ACT.Ln, scale=math.exp(0.5))
+            nc.vector.scalar_tensor_tensor(
+                den[:, slots], x[:, slots], 0.5, soft[:, slots], ALU.add, ALU.max
+            )
+        log_den = pool.tile([P, I], F32, name="log_den")
+        for slots in rest:
+            nc.scalar.activation(log_den[:, slots], den[:, slots], ACT.Ln)
+
+        def put(slots, inv):
+            nc.vector.tensor_tensor(f1[:].indirect(entries(list_w, slots)), top[:, slots], inv, ALU.mult)
+
+        inv_first = pool.tile([P, DIVIDED], F32, name="inv_first")
+        nc.vector.reciprocal(inv_first[:], den[:, first])
+        put(first, inv_first[:])
+        centre = slice(256, 384)
+        inv_centre = pool.tile([P, 128], F32, name="inv_centre")
+        nc.scalar.activation(inv_centre[:], log_den[:, centre], ACT.Exp, scale=-1.0)
+        put(centre, inv_centre[:])
+        inv_outer = pool.tile([P, 2, 128], F32, name="inv_outer")
+        outer = log_den[:].rearrange("p (u v c) -> p u v c", u=2, v=2)[:, :, 1, :]
+        nc.scalar.activation(inv_outer[:], outer, ACT.Exp, scale=-1.0)
+        put(slice(128, 256), inv_outer[:, 0, :])
+        put(slice(384, 512), inv_outer[:, 1, :])
+
+        for t0 in range(0, T, OUT_PIECE):
+            cols = slice(t0, t0 + OUT_PIECE)
+            nc.vector.tensor_tensor(total[:, cols], total[:, cols], f1[:, cols], ALU.add)
+            nc.sync.dma_start(out=out[:, cols], in_=total[:, cols])

@@ -1,5 +1,6 @@
 import math
 from contextlib import ExitStack
+from itertools import accumulate
 
 import concourse.mybir as mybir
 
@@ -20,11 +21,11 @@ ACT = mybir.ActivationFunctionType
 P = 128
 PACK = 4
 LANES = 16
-EXP_CAP = 2.0**57
+LINEAR_FROM = 40.0
 DIVIDED = 128
-B_PIECE = 256
-A_PIECE = 512
-OUT_PIECE = 256
+B_PIECES = [256, 256, 256, 128, 128]
+A_PIECES = [512, 512]
+OUT_PIECES = [384, 384, 128, 128]
 
 
 def tile_attend_worthfor_lean_putold_heads_kernel(
@@ -39,25 +40,25 @@ def tile_attend_worthfor_lean_putold_heads_kernel(
             return lists[:, slots.start // LANES : slots.stop // LANES]
 
         key_scales = pool.tile([P, T], U8, name="key_scales", align_bytes=64)
-        nc.vector.memset(key_scales[:].bitcast(I32), 0)
+        nc.gpsimd.memset(key_scales[:].bitcast(I32), 0)
         f1 = pool.tile([P, T], F32, name="f1")
         nc.vector.memset(f1[:], 0.0)
 
         raw2 = pool.tile([P, PACK, Q], F32, name="raw2")
         nc.sync.dma_start(out=raw2[:], in_=query2.rearrange("(p j) q -> p j q", j=PACK))
+        key_words = pool.tile([P, 2 * T], U8, name="key_words", align_bytes=64)
+        nc.sync.dma_start(out=key_words[:].bitcast(I32), in_=keys_words[0].bitcast(I32))
         for quad in range(4):
-            nc.scalar.dma_start(
+            nc.sync.dma_start(
                 out=key_scales[32 * quad : 32 * quad + 4, :].bitcast(I32),
                 in_=keys_scales[0, 4 * quad : 4 * quad + 4, :].bitcast(I32),
             )
-        key_words = pool.tile([P, 2 * T], U8, name="key_words", align_bytes=64)
-        nc.sync.dma_start(out=key_words[:].bitcast(I32), in_=keys_words[0].bitcast(I32))
         raw1 = pool.tile([P, PACK, Q], F32, name="raw1")
         nc.sync.dma_start(out=raw1[:], in_=query.rearrange("(p j) q -> p j q", j=PACK))
         list_b = pool.tile([P, I // LANES], U16, name="list_b")
         nc.sync.dma_start(list_b[:], offs2)
         lam_col = pool.tile([P, 1], F32, name="lam_col")
-        nc.gpsimd.dma_start(out=lam_col[:], in_=lam)
+        nc.sync.dma_start(out=lam_col[:], in_=lam)
         list_a = pool.tile([P, I // LANES], U16, name="list_a")
         nc.sync.dma_start(list_a[:], offs)
         list_w = pool.tile([P, I // LANES], U16, name="list_w")
@@ -65,12 +66,15 @@ def tile_attend_worthfor_lean_putold_heads_kernel(
         total = pool.tile([P, T], F32, name="total")
         nc.sync.dma_start(out=total[:], in_=old)
 
-        def quantize(raw, name):
+        def quantize(raw, name, copies):
             grouped = pool.tile([P, Q, PACK], BF16, name=name + "_grouped", align_bytes=64)
-            nc.vector.tensor_copy(
-                out=grouped[:].rearrange("p (c i) j -> p c j i", i=4),
-                in_=raw[:].rearrange("p j (c i) -> p c j i", i=4),
-            )
+            share = Q // len(copies)
+            for n, copy in enumerate(copies):
+                cols = slice(n * share, (n + 1) * share)
+                copy(
+                    out=grouped[:, cols, :].rearrange("p (c i) j -> p c j i", i=4),
+                    in_=raw[:, :, cols].rearrange("p j (c i) -> p c j i", i=4),
+                )
             codes = pool.tile([P, Q], U32, name=name + "_codes", align_bytes=64)
             scales = pool.tile([P, Q], U8, name=name + "_scales", align_bytes=64)
             nc.vector.quantize_mx(
@@ -80,10 +84,10 @@ def tile_attend_worthfor_lean_putold_heads_kernel(
             )
             return codes, scales
 
-        def scores(codes, scales, piece, name, copy):
+        def scores(codes, scales, pieces, name, copy, banks):
             whole = pool.tile([P, T], F32, name=name)
-            for t0 in range(0, T, piece):
-                bank = psum.tile([P, piece], F32, name=f"{name}_bank{t0}")
+            for t0, piece, tag in zip(accumulate([0] + pieces), pieces, banks):
+                bank = psum.tile([P, piece], F32, name=f"{name}_bank{t0}", tag=tag)
                 nc.tensor.matmul_mx(
                     out=bank[:],
                     lhsT=codes[:].bitcast(FP8X4),
@@ -96,63 +100,56 @@ def tile_attend_worthfor_lean_putold_heads_kernel(
                 copy(out=whole[:, t0 : t0 + piece], in_=bank[:])
             return whole
 
-        codes2, scales2 = quantize(raw2, "q2")
-        codes1, scales1 = quantize(raw1, "q1")
-        b = scores(codes2, scales2, B_PIECE, "b", nc.scalar.copy)
+        codes2, scales2 = quantize(raw2, "q2", [nc.vector.tensor_copy, nc.scalar.copy])
+        codes1, scales1 = quantize(raw1, "q1", [nc.vector.tensor_copy])
+        b = scores(codes2, scales2, B_PIECES, "b", nc.scalar.copy, ["p0", "p1", "p2", "p3", "p4"])
 
         half = I // 2
         halves = [slice(0, half), slice(half, I)]
-        lam_rows = pool.tile([P, half], F32, name="lam_rows")
-        nc.vector.tensor_copy(out=lam_rows[:], in_=lam_col[:].to_broadcast([P, half]))
+        lam_rows = pool.tile([P, I], F32, name="lam_rows")
+        nc.gpsimd.tensor_scalar(lam_rows[:], lam_col[:].to_broadcast([P, I]), 1.0, 0.0, ALU.mult, ALU.add)
 
         x = pool.tile([P, I], F32, name="x")
-        nc.scalar.activation(x[:, halves[0]], b[:].indirect(entries(list_b, halves[0])), ACT.Copy)
-        nc.vector.tensor_copy(x[:, halves[1]], b[:].indirect(entries(list_b, halves[1])))
+        nc.scalar.activation(x[:, halves[0]], b[:].indirect(entries(list_b, halves[0])), ACT.Copy, bias=0.5)
+        nc.vector.tensor_scalar(
+            x[:, halves[1]], b[:].indirect(entries(list_b, halves[1])), 1.0, 0.5, ALU.mult, ALU.add
+        )
         e = pool.tile([P, I], F32, name="e")
         nc.scalar.activation(e[:], x[:], ACT.Exp)
 
-        a = scores(codes1, scales1, A_PIECE, "a", nc.vector.tensor_copy)
+        a = scores(codes1, scales1, A_PIECES, "a", nc.vector.tensor_copy, ["p3", "p4"])
 
-        capped = pool.tile([P, I], F32, name="capped")
-        nc.vector.tensor_scalar(capped[:], e[:], EXP_CAP, 1.0, ALU.min, ALU.add)
-
-        top = e
-        for slots in halves:
-            nc.vector.tensor_tensor(
-                top[:, slots], a[:].indirect(entries(list_a, slots)), lam_rows[:], ALU.mult
-            )
+        top = pool.tile([P, I], F32, name="top")
+        nc.vector.tensor_tensor(top[:], a[:].indirect(list_a[:]), lam_rows[:], ALU.mult)
 
         first = slice(0, DIVIDED)
+        rest = slice(DIVIDED, I)
         mid = (DIVIDED + I) // 2
-        rest = [slice(DIVIDED, mid), slice(mid, I)]
+        rest_halves = [slice(DIVIDED, mid), slice(mid, I)]
         soft = pool.tile([P, I], F32, name="soft")
-        den = pool.tile([P, I], F32, name="den")
-        for slots in rest + [first]:
-            nc.scalar.activation(soft[:, slots], capped[:, slots], ACT.Ln, scale=math.exp(0.5))
+        den = lam_rows
+        for slots in rest_halves + [first]:
+            nc.scalar.activation(soft[:, slots], e[:, slots], ACT.Ln, bias=math.exp(0.5))
             nc.vector.scalar_tensor_tensor(
-                den[:, slots], x[:, slots], 0.5, soft[:, slots], ALU.add, ALU.max
+                den[:, slots], soft[:, slots], LINEAR_FROM, x[:, slots], ALU.min, ALU.max
             )
         log_den = pool.tile([P, I], F32, name="log_den")
-        for slots in rest:
+        for slots in rest_halves:
             nc.scalar.activation(log_den[:, slots], den[:, slots], ACT.Ln)
 
-        def put(slots, inv):
-            nc.vector.tensor_tensor(f1[:].indirect(entries(list_w, slots)), top[:, slots], inv, ALU.mult)
+        inv = pool.tile([P, I], F32, name="inv")
 
-        inv_first = pool.tile([P, DIVIDED], F32, name="inv_first")
-        nc.vector.reciprocal(inv_first[:], den[:, first])
-        put(first, inv_first[:])
-        centre = slice(256, 384)
-        inv_centre = pool.tile([P, 128], F32, name="inv_centre")
-        nc.scalar.activation(inv_centre[:], log_den[:, centre], ACT.Exp, scale=-1.0)
-        put(centre, inv_centre[:])
-        inv_outer = pool.tile([P, 2, 128], F32, name="inv_outer")
-        outer = log_den[:].rearrange("p (u v c) -> p u v c", u=2, v=2)[:, :, 1, :]
-        nc.scalar.activation(inv_outer[:], outer, ACT.Exp, scale=-1.0)
-        put(slice(128, 256), inv_outer[:, 0, :])
-        put(slice(384, 512), inv_outer[:, 1, :])
+        def put(slots):
+            nc.vector.tensor_tensor(
+                f1[:].indirect(entries(list_w, slots)), top[:, slots], inv[:, slots], ALU.mult
+            )
 
-        for t0 in range(0, T, OUT_PIECE):
-            cols = slice(t0, t0 + OUT_PIECE)
+        nc.vector.reciprocal(inv[:, first], den[:, first])
+        put(first)
+        nc.scalar.activation(inv[:, rest], log_den[:, rest], ACT.Exp, scale=-1.0)
+        put(rest)
+
+        for t0, piece in zip(accumulate([0] + OUT_PIECES), OUT_PIECES):
+            cols = slice(t0, t0 + piece)
             nc.vector.tensor_tensor(total[:, cols], total[:, cols], f1[:, cols], ALU.add)
             nc.sync.dma_start(out=out[:, cols], in_=total[:, cols])

@@ -25,7 +25,7 @@ LINEAR_FROM = 40.0
 DIVIDED = 128
 B_PIECES = [256, 256, 256, 128, 128]
 A_PIECES = [512, 512]
-OUT_PIECES = [384, 384, 128, 128]
+OUT_PIECES = [256, 256, 256, 256]
 
 
 def tile_attend_worthfor_lean_putold_heads_kernel(
@@ -117,7 +117,7 @@ def tile_attend_worthfor_lean_putold_heads_kernel(
         e = pool.tile([P, I], F32, name="e")
         nc.scalar.activation(e[:], x[:], ACT.Exp)
 
-        a = scores(codes1, scales1, A_PIECES, "a", nc.vector.tensor_copy, ["p3", "p4"])
+        a = scores(codes1, scales1, A_PIECES, "a", nc.vector.tensor_copy, ["p2", "p3"])
 
         top = pool.tile([P, I], F32, name="top")
         nc.vector.tensor_tensor(top[:], a[:].indirect(list_a[:]), lam_rows[:], ALU.mult)
@@ -128,26 +128,25 @@ def tile_attend_worthfor_lean_putold_heads_kernel(
         rest_halves = [slice(DIVIDED, mid), slice(mid, I)]
         soft = pool.tile([P, I], F32, name="soft")
         den = lam_rows
-        for slots in rest_halves + [first]:
+        for slots in [first] + rest_halves:
             nc.scalar.activation(soft[:, slots], e[:, slots], ACT.Ln, bias=math.exp(0.5))
             nc.vector.scalar_tensor_tensor(
                 den[:, slots], soft[:, slots], LINEAR_FROM, x[:, slots], ALU.min, ALU.max
             )
-        log_den = pool.tile([P, I], F32, name="log_den")
+
+        def put(slots, inv):
+            nc.vector.tensor_tensor(f1[:].indirect(entries(list_w, slots)), top[:, slots], inv, ALU.mult)
+
+        inv_first = soft[:, DIVIDED : 2 * DIVIDED]
+        nc.vector.reciprocal(inv_first, den[:, first])
+        put(first, inv_first)
+        root = pool.tile([P, I], F32, name="root")
+        inv_rest = pool.tile([P, I], F32, name="inv_rest")
         for slots in rest_halves:
-            nc.scalar.activation(log_den[:, slots], den[:, slots], ACT.Ln)
-
-        inv = pool.tile([P, I], F32, name="inv")
-
-        def put(slots):
-            nc.vector.tensor_tensor(
-                f1[:].indirect(entries(list_w, slots)), top[:, slots], inv[:, slots], ALU.mult
-            )
-
-        nc.vector.reciprocal(inv[:, first], den[:, first])
-        put(first)
-        nc.scalar.activation(inv[:, rest], log_den[:, rest], ACT.Exp, scale=-1.0)
-        put(rest)
+            nc.scalar.activation(root[:, slots], den[:, slots], ACT.Abs_reciprocal_sqrt)
+        for slots in rest_halves:
+            nc.scalar.activation(inv_rest[:, slots], root[:, slots], ACT.Square)
+        put(rest, inv_rest[:, rest])
 
         for t0, piece in zip(accumulate([0] + OUT_PIECES), OUT_PIECES):
             cols = slice(t0, t0 + piece)

import math
from contextlib import ExitStack
from itertools import accumulate

import concourse.mybir as mybir

D, T, I, Q = 512, 1024, 512, 128
FLOPS = 2 * 2 * D * T * Q

F32 = mybir.dt.float32
BF16 = mybir.dt.bfloat16
I32 = mybir.dt.int32
U32 = mybir.dt.uint32
U16 = mybir.dt.uint16
U8 = mybir.dt.uint8
FP8X4 = mybir.dt.float8_e4m3fn_x4
FP4X4 = mybir.dt.float4_e2m1fn_x4
ALU = mybir.AluOpType
ACT = mybir.ActivationFunctionType

P = 128
PACK = 4
LANES = 16
LINEAR_FROM = 40.0
DIVIDED = 128
B_PIECES = [256, 256, 256, 128, 128]
A_PIECES = [512, 512]
OUT_PIECES = [256, 256, 256, 256]


def tile_attend_worthfor_lean_putold_heads_kernel(
    tc, query, query2, keys_words, keys_scales, lam, old, offs, offs2, offs3, out
):
    nc = tc.nc
    with ExitStack() as ctx:
        pool = ctx.enter_context(tc.tile_pool(name="sbuf", bufs=1))
        psum = ctx.enter_context(tc.psum_pool(name="psum", bufs=1))

        def entries(lists, slots):
            return lists[:, slots.start // LANES : slots.stop // LANES]

        key_scales = pool.tile([P, T], U8, name="key_scales", align_bytes=64)
        nc.gpsimd.memset(key_scales[:].bitcast(I32), 0)
        f1 = pool.tile([P, T], F32, name="f1")
        nc.vector.memset(f1[:], 0.0)

        raw2 = pool.tile([P, PACK, Q], F32, name="raw2")
        nc.sync.dma_start(out=raw2[:], in_=query2.rearrange("(p j) q -> p j q", j=PACK))
        key_words = pool.tile([P, 2 * T], U8, name="key_words", align_bytes=64)
        nc.sync.dma_start(out=key_words[:].bitcast(I32), in_=keys_words[0].bitcast(I32))
        for quad in range(4):
            nc.sync.dma_start(
                out=key_scales[32 * quad : 32 * quad + 4, :].bitcast(I32),
                in_=keys_scales[0, 4 * quad : 4 * quad + 4, :].bitcast(I32),
            )
        raw1 = pool.tile([P, PACK, Q], F32, name="raw1")
        nc.sync.dma_start(out=raw1[:], in_=query.rearrange("(p j) q -> p j q", j=PACK))
        list_b = pool.tile([P, I // LANES], U16, name="list_b")
        nc.sync.dma_start(list_b[:], offs2)
        lam_col = pool.tile([P, 1], F32, name="lam_col")
        nc.sync.dma_start(out=lam_col[:], in_=lam)
        list_a = pool.tile([P, I // LANES], U16, name="list_a")
        nc.sync.dma_start(list_a[:], offs)
        list_w = pool.tile([P, I // LANES], U16, name="list_w")
        nc.sync.dma_start(list_w[:], offs3)
        total = pool.tile([P, T], F32, name="total")
        nc.sync.dma_start(out=total[:], in_=old)

        def quantize(raw, name, copies):
            grouped = pool.tile([P, Q, PACK], BF16, name=name + "_grouped", align_bytes=64)
            share = Q // len(copies)
            for n, copy in enumerate(copies):
                cols = slice(n * share, (n + 1) * share)
                copy(
                    out=grouped[:, cols, :].rearrange("p (c i) j -> p c j i", i=4),
                    in_=raw[:, :, cols].rearrange("p j (c i) -> p c j i", i=4),
                )
            codes = pool.tile([P, Q], U32, name=name + "_codes", align_bytes=64)
            scales = pool.tile([P, Q], U8, name=name + "_scales", align_bytes=64)
            nc.vector.quantize_mx(
                out=codes[:].bitcast(FP8X4),
                scales=scales[:],
                in_=grouped[:].rearrange("p q j -> p (q j)"),
            )
            return codes, scales

        def scores(codes, scales, pieces, name, copy, banks):
            whole = pool.tile([P, T], F32, name=name)
            for t0, piece, tag in zip(accumulate([0] + pieces), pieces, banks):
                bank = psum.tile([P, piece], F32, name=f"{name}_bank{t0}", tag=tag)
                nc.tensor.matmul_mx(
                    out=bank[:],
                    lhsT=codes[:].bitcast(FP8X4),
                    lhsT_scale=scales[:],
                    rhs=key_words[:, 2 * t0 : 2 * (t0 + piece)].bitcast(FP4X4),
                    rhs_scale=key_scales[:, t0 : t0 + piece],
                    start=True,
                    stop=True,
                )
                copy(out=whole[:, t0 : t0 + piece], in_=bank[:])
            return whole

        codes2, scales2 = quantize(raw2, "q2", [nc.vector.tensor_copy, nc.scalar.copy])
        codes1, scales1 = quantize(raw1, "q1", [nc.vector.tensor_copy])
        b = scores(codes2, scales2, B_PIECES, "b", nc.scalar.copy, ["p0", "p1", "p2", "p3", "p4"])

        half = I // 2
        halves = [slice(0, half), slice(half, I)]
        lam_rows = pool.tile([P, I], F32, name="lam_rows")
        nc.gpsimd.tensor_scalar(lam_rows[:], lam_col[:].to_broadcast([P, I]), 1.0, 0.0, ALU.mult, ALU.add)

        x = pool.tile([P, I], F32, name="x")
        nc.scalar.activation(x[:, halves[0]], b[:].indirect(entries(list_b, halves[0])), ACT.Copy, bias=0.5)
        nc.vector.tensor_scalar(
            x[:, halves[1]], b[:].indirect(entries(list_b, halves[1])), 1.0, 0.5, ALU.mult, ALU.add
        )
        e = pool.tile([P, I], F32, name="e")
        nc.scalar.activation(e[:], x[:], ACT.Exp)

        a = scores(codes1, scales1, A_PIECES, "a", nc.vector.tensor_copy, ["p2", "p3"])

        top = pool.tile([P, I], F32, name="top")
        nc.vector.tensor_tensor(top[:], a[:].indirect(list_a[:]), lam_rows[:], ALU.mult)

        first = slice(0, DIVIDED)
        rest = slice(DIVIDED, I)
        mid = (DIVIDED + I) // 2
        rest_halves = [slice(DIVIDED, mid), slice(mid, I)]
        soft = pool.tile([P, I], F32, name="soft")
        den = lam_rows
        for slots in [first] + rest_halves:
            nc.scalar.activation(soft[:, slots], e[:, slots], ACT.Ln, bias=math.exp(0.5))
            nc.vector.scalar_tensor_tensor(
                den[:, slots], soft[:, slots], LINEAR_FROM, x[:, slots], ALU.min, ALU.max
            )

        def put(slots, inv):
            nc.vector.tensor_tensor(f1[:].indirect(entries(list_w, slots)), top[:, slots], inv, ALU.mult)

        inv_first = soft[:, DIVIDED : 2 * DIVIDED]
        nc.vector.reciprocal(inv_first, den[:, first])
        put(first, inv_first)
        root = pool.tile([P, I], F32, name="root")
        inv_rest = pool.tile([P, I], F32, name="inv_rest")
        for slots in rest_halves:
            nc.scalar.activation(root[:, slots], den[:, slots], ACT.Abs_reciprocal_sqrt)
        for slots in rest_halves:
            nc.scalar.activation(inv_rest[:, slots], root[:, slots], ACT.Square)
        put(rest, inv_rest[:, rest])

        for t0, piece in zip(accumulate([0] + OUT_PIECES), OUT_PIECES):
            cols = slice(t0, t0 + piece)
            nc.vector.tensor_tensor(total[:, cols], total[:, cols], f1[:, cols], ALU.add)
            nc.sync.dma_start(out=out[:, cols], in_=total[:, cols])
